import numpy as np
import ml_dtypes


def mxq(x, axis, fmt="e4m3"):
    dtype, down = {"e4m3": (ml_dtypes.float8_e4m3fn, 7), "e5m2": (ml_dtypes.float8_e5m2, 14)}[fmt]
    v = np.moveaxis(np.asarray(x, np.float32).astype(ml_dtypes.bfloat16).astype(np.float64), axis, -1)
    blocks = v.reshape(v.shape[:-1] + (-1, 32))
    amax = np.abs(blocks).max(-1, keepdims=True)
    byte = np.maximum(np.where(amax > 0, np.frexp(amax)[1] - 1 + 127, 0) - down, 1)
    scale = np.exp2(byte - 127.0)
    codes = (blocks / scale).astype(np.float32).astype(dtype).astype(np.float64)
    return np.moveaxis((codes * scale).reshape(v.shape), -1, axis)


WIDE = False


def mx_kscale(k):
    if not WIDE:
        return np.ones(k)
    levels = np.array([10, -10, 5, -5, 0])
    if k % 512:
        return np.exp2(np.random.permutation(np.resize(levels, k // 32))).repeat(32)
    a = np.empty((k // 512, 16))
    for p in range(k // 512):
        a[p, :8] = np.random.permutation(np.resize(levels, 8))
        for g in range(8):
            far = levels[np.abs(levels - a[p, g]) >= 10]
            a[p, g + 8] = far[np.random.randint(len(far))]
    return np.exp2(a.ravel()).repeat(32)


def f64(x):
    return np.asarray(x).astype(np.float64)


def striped(idx):
    return np.tile(idx.reshape(-1, 16).T, (8, 1)).astype(np.uint16)


def unstriped(offs):
    return offs[:16].T.reshape(-1).astype(np.int64)


def striped8(idx):
    return np.concatenate([x.reshape(-1, 16).T for x in idx]).astype(np.uint16)


def runs(offs, k):
    lists = np.stack([offs[16 * r : 16 * r + 16].T.reshape(-1) for r in range(8)]).astype(np.int64)
    return lists[np.arange(k) % 512 // 64]


def pack_weight(w):
    k, n = w.shape
    w = f64(np.asarray(w, np.float32).astype(ml_dtypes.bfloat16)).reshape(k // 32, 32, n)
    amax = np.abs(w).max(1)
    byte = np.clip(np.where(amax > 0, np.frexp(amax)[1] - 1 + 127 - 7, 1), 1, 254)
    scaled = (w * np.exp2(127.0 - byte)[:, None, :]).reshape(k, n).astype(np.float32)
    words = np.ascontiguousarray(scaled.reshape(k // 512, 128, 4, n).transpose(0, 1, 3, 2)).astype(ml_dtypes.float8_e4m3fn).view(np.uint8)
    return words, np.ascontiguousarray(byte.astype(np.uint8).reshape(k // 512, 16, n))


def unpack_weight(words, scales):
    g, p, n, _ = words.shape
    vals = np.ascontiguousarray(words).view(ml_dtypes.float8_e4m3fn).astype(np.float64) * np.repeat(np.exp2(scales.astype(np.float64) - 127.0), 8, axis=1)[..., None]
    return vals.transpose(0, 1, 3, 2).reshape(g * 512, n)


def relu(v):
    return np.maximum(v, 0.0)

def planes(y):
    n, m = y.shape
    v = y.astype(np.float32).astype(ml_dtypes.bfloat16).astype(np.float64).reshape(n // 32, 32, m)
    top = np.abs(v).max(1)
    byte = np.clip(np.where(top > 0, np.frexp(top)[1] - 1 + 127 - 7, 1), 1, 254)
    codes = (v * np.exp2(127.0 - byte)[:, None, :]).reshape(n, m).astype(np.float32).astype(ml_dtypes.float8_e4m3fn).view(np.uint8)
    words = codes.reshape(n // 512, 128, 4, m).transpose(0, 1, 3, 2)
    return np.ascontiguousarray(words), np.ascontiguousarray(byte.astype(np.uint8).reshape(n // 512, 16, m))


K, T, S, N, G, H = 512, 1024, 512, 512, 2048, 512


def setup_inputs():
    n = np.random.standard_normal
    s = mx_kscale(K)[:, None]
    u = mx_kscale(S)
    packed_xT = pack_weight(n((K, T)) * s)
    packed_dT = pack_weight(n((K, G)) / s)
    packed_w1 = pack_weight(n((H, N)) / np.sqrt(H) / u[:, None])
    return {
        "x_words": packed_xT[0],
        "x_scales": packed_xT[1],
        "d_words": packed_dT[0],
        "d_scales": packed_dT[1],
        "gn": (np.random.uniform(0.5, 1.5, (H, 1)) * u[:, None]).astype(np.float32),
        "w1_words": packed_w1[0],
        "w1_scales": packed_w1[1],
        "offs": striped(np.random.permutation(T)[:S]),
        "k1": striped8(np.random.randint(0, G, (8, H))),
        "two": striped(np.random.permutation(T)[:S]),
        "k2": striped8(np.random.randint(0, G, (8, H))),
        "n1": striped(np.random.permutation(S)),
        "n2": striped(np.random.permutation(S)),
        "n3": striped(np.random.permutation(S)),
        "n4": striped8(np.stack([np.random.permutation(S) for _ in range(8)])),
        "n5": striped8(np.stack([np.random.permutation(S) for _ in range(8)])),
    }


def reference(x_words, x_scales, d_words, d_scales, gn, w1_words, w1_scales, offs, k1, two, k2, n1, n2, n3, n4, n5):
    d_k1 = unpack_weight(d_words, d_scales)[np.arange(K)[:, None], runs(k1, K)]
    xq = unpack_weight(x_words, x_scales)[:, unstriped(offs)]
    a = 0.0625 * (d_k1.T @ xq)
    d_k2 = unpack_weight(d_words, d_scales)[np.arange(K)[:, None], runs(k2, K)]
    x_two = unpack_weight(x_words, x_scales)[:, unstriped(two)]
    b = 0.0625 * (d_k2.T @ x_two)
    z = f64(gn) * (np.maximum(np.minimum(a - (0.5 * a[:, unstriped(n1)]), b[:, unstriped(n2)]), b[:, unstriped(n3)]))
    h = unpack_weight(w1_words, w1_scales).T @ mxq(z, 0, "e4m3")
    pa = h - (h[np.arange(N)[:, None], runs(n4, N)])
    pb = h[np.arange(N)[:, None], runs(n5, N)] - h
    out_0 = relu(np.minimum(pa, pb)) - (relu(-1.0 * np.maximum(pa, pb)))
    return (out_0,) + planes(out_0)

@@ -1,0 +1,212 @@
+from contextlib import ExitStack
+
+import concourse.mybir as mybir
+
+F32 = mybir.dt.float32
+BF16 = mybir.dt.bfloat16
+U32 = mybir.dt.uint32
+I32 = mybir.dt.int32
+U16 = mybir.dt.uint16
+U8 = mybir.dt.uint8
+FP8X4 = mybir.dt.float8_e4m3fn_x4
+ALU = mybir.AluOpType
+COPY = mybir.ActivationFunctionType.Copy
+
+P = 128
+PACK = 4
+S = 512
+T = 1024
+G = 2048
+HALF = 256
+WIDE = 384
+PAD = 32
+FLOPS = 3 * 2 * 512 * 512 * 512
+
+
+def tile_picked_twpqclampbminmod_none_po_kernel(tc, x_words, x_scales, d_words, d_scales, gn, w1_words, w1_scales,
+        offs, k1, two, k2, n1, n2, n3, n4, n5, out_0, out_1, out_2):
+    nc = tc.nc
+    with ExitStack() as ctx:
+        keep = ctx.enter_context(tc.tile_pool(name="keep", bufs=1))
+        psum = ctx.enter_context(tc.psum_pool(name="psum", bufs=1))
+
+        def sb(name, shape, dtype, tag=None):
+            return keep.tile(shape, dtype, name=name, tag=tag or name, align_bytes=64)
+
+        def load_list(name, src):
+            tile = sb(name, [P, S // 16], U16)
+            nc.sync.dma_start(tile[:], src)
+            return tile
+
+        def load_words(name, src, cols, tag=None):
+            tile = sb(name, [P, cols], U32, tag)
+            nc.sync.dma_start(tile[:].bitcast(I32), src[0].rearrange("p n t -> p (n t)").bitcast(I32))
+            return tile
+
+        def load_scale_rows(name, src, cols):
+            tile = sb(name, [P, cols], U8)
+            rows = src[0].bitcast(I32).unsqueeze(1).broadcast_to([16, 8, cols // 4])
+            nc.sync.dma_start(tile[:].bitcast(I32), rows)
+            return tile
+
+        def deal_words(dst, src):
+            nc.vector.tensor_copy(dst.rearrange("p (t c i) -> p c t i", t=PACK, i=4),
+                                  src.rearrange("p (c i t) -> p c t i", t=PACK, i=4))
+
+        def deal_bytes(dst, src):
+            nc.vector.tensor_copy(dst.rearrange("p (t m) -> p t m", t=PACK),
+                                  src.rearrange("p (m t) -> p t m", t=PACK))
+
+        planes = [sb("plane%d" % e, [P, 2 * S], U8) for e in range(2)]
+        w_rows = sb("w_rows", [P, S], U8)
+        for tile in planes + [w_rows]:
+            nc.gpsimd.memset(tile[:].bitcast(I32), 0)
+
+        a = [sb("a%d" % t, [P, S + PAD], F32) for t in range(PACK)]
+        b = [sb("b%d" % t, [P, S], F32) for t in range(PACK)]
+        for t in range(PACK):
+            nc.gpsimd.memset(a[t][:, S:], 0.0)
+
+        offs_l = load_list("offs_l", offs)
+        x_rows = load_scale_rows("x_rows", x_scales, T)
+        k1_l = load_list("k1_l", k1)
+        d_rows = load_scale_rows("d_rows", d_scales, G)
+        x_tab = load_words("x_tab", x_words, T)
+        k2_l = load_list("k2_l", k2)
+        two_l = load_list("two_l", two)
+        n1_l = load_list("n1_l", n1)
+        n2_l = load_list("n2_l", n2)
+        d_tab = load_words("d_tab", d_words, G)
+        n3_l = load_list("n3_l", n3)
+        n4_l = load_list("n4_l", n4)
+        n5_l = load_list("n5_l", n5)
+
+        gain_raw = sb("gain_raw", [P, PACK], F32)
+        nc.gpsimd.dma_start(gain_raw[:], gn.rearrange("(p t) o -> p (t o)", t=PACK))
+        for q in range(4):
+            nc.gpsimd.dma_start(w_rows[32 * q:32 * q + 4, :].bitcast(I32), w1_scales[0, 4 * q:4 * q + 4, :].bitcast(I32))
+        gain = sb("gain", [P, PACK], F32)
+        nc.scalar.activation(gain[:], gain_raw[:], COPY, scale=0.0625)
+
+        def coded_product(e, k_l, x_l, rows, on_vector):
+            plane = planes[e]
+            g_b = sb("g_b%d" % e, [P, 2 * S], U8, "chain" if e else None)
+            side = sb("side%d" % e, [P, 2 * S], U8)
+            nc.vector.tensor_copy(g_b[:, S:], x_rows[:].indirect(x_l[:]))
+            nc.vector.tensor_copy(g_b[:, :S], d_rows[:].indirect(k_l[:]))
+            nc.vector.tensor_copy(side[:, S:].bitcast(I32), g_b[:, S:].bitcast(I32))
+            deal_bytes(side[:, :S], g_b[:, :S])
+            for q in range(4):
+                nc.sync.dma_start(plane[32 * q:32 * q + 4, :].bitcast(I32),
+                                  side[32 * q:32 * q + 32:8, :].bitcast(I32))
+            if e == 0:
+                gx_w = sb("gx_w0", [P, S], U32)[:]
+                gd_w = sb("gd_w0", [P, S], U32, "chain")[:]
+            else:
+                g_w = sb("g_w1", [P, 2 * S], U32, "chain")
+                gx_w, gd_w = g_w[:, S:], g_w[:, :S]
+            dealt = sb("dealt%d" % e, [P, S], U32)
+            nc.vector.tensor_copy(gx_w, x_tab[:].indirect(x_l[:]))
+            nc.vector.tensor_copy(gd_w, d_tab[:].indirect(k_l[:]))
+            deal_words(dealt[:], gd_w)
+            for t in range(PACK):
+                cols = slice(P * t, P * (t + 1))
+                acc = psum.tile([P, S], F32, name="acc", tag="bank%d" % (PACK * e + t))
+                nc.tensor.matmul_mx(acc[:], lhsT=dealt[:, cols].bitcast(FP8X4), lhsT_scale=plane[:, cols],
+                                    rhs=gx_w.bitcast(FP8X4), rhs_scale=plane[:, S:], start=True, stop=True)
+                if t in on_vector:
+                    nc.vector.tensor_copy(rows[t][:, :S], acc[:])
+                else:
+                    nc.scalar.copy(rows[t][:, :S], acc[:])
+
+        def fetch(engine, dst, window, list_tile, cols):
+            picked = window[:].indirect(list_tile[:, cols.start // 16:cols.stop // 16])
+            if engine == "v":
+                nc.vector.tensor_copy(dst, picked)
+            else:
+                nc.scalar.activation(dst, picked, COPY)
+
+        coded_product(0, k1_l, offs_l, a, ())
+        a1 = sb("a_at_n1", [P, PACK, S], F32)
+        for t in range(PACK):
+            fetch("s", a1[:, t, :], a[t], n1_l, slice(0, S))
+        coded_product(1, k2_l, two_l, b, (0, 1))
+
+        w_tab = load_words("w_tab", w1_words, S, "g_b0")
+        w_codes = sb("w_codes", [P, S], U32, "dealt0")
+        w_plane = sb("w_plane", [P, S], U8, "plane0")
+        deal_words(w_codes[:], w_tab[:])
+        deal_bytes(w_plane[:], w_rows[:])
+
+        u = sb("u", [P, PACK, S], F32)
+        for t in range(PACK):
+            nc.vector.scalar_tensor_tensor(u[:, t, :], a1[:, t, :], -0.5, a[t][:, :S], ALU.mult, ALU.add)
+
+        hid = [sb("hid%d" % t, [P, S], F32) for t in range(PACK)]
+        z_codes = sb("z_codes", [P, S], U32)
+        z_plane = sb("z_plane", [P, S], U8)
+        groups = [(slice(0, 256), (0, 1)), (slice(0, 256), (2, 3)), (slice(256, 384), (0, 1, 2, 3)), (slice(384, 512), (0, 1, 2, 3))]
+        banks = {}
+        for piece, cols in enumerate((slice(0, WIDE), slice(WIDE, S))):
+            n = cols.stop - cols.start
+            b2 = sb("b2_%d" % piece, [P, PACK, n], F32)
+            b3 = sb("b3_%d" % piece, [P, PACK, n], F32)
+            low = sb("low%d" % piece, [P, PACK, n], F32)
+            top = sb("top%d" % piece, [P, PACK, n], F32)
+            for ts in ((slice(0, 2), slice(2, 4)) if piece == 0 else (slice(0, 4),)):
+                for t in range(ts.start, ts.stop):
+                    fetch("v" if (piece, t) == (0, 0) else "s", b2[:, t, :], b[t], n2_l, cols)
+                for t in range(ts.start, ts.stop):
+                    fetch("v" if (piece, t) == (0, 0) else "s", b3[:, t, :], b[t], n3_l, cols)
+                nc.vector.tensor_tensor(low[:, ts, :], u[:, ts, cols], b2[:, ts, :], ALU.min)
+                nc.vector.tensor_tensor(top[:, ts, :], low[:, ts, :], b3[:, ts, :], ALU.max)
+            z = sb("z%d" % piece, [P, n * PACK], BF16)
+            nc.vector.tensor_tensor(z[:].rearrange("p (c i t) -> p c t i", i=4, t=PACK),
+                                    top[:].rearrange("p t (c i) -> p c t i", i=4),
+                                    gain[:].unsqueeze(1).unsqueeze(3).broadcast_to([P, n // 4, PACK, 4]), ALU.mult)
+            nc.vector.quantize_mx(z_codes[:, cols].bitcast(FP8X4), z_plane[:, cols], z[:])
+            for g, (gc, tiles) in enumerate(groups):
+                if cols.start <= gc.start and gc.stop <= cols.stop:
+                    banks[g] = psum.tile([P, len(tiles), gc.stop - gc.start], F32, name="acc_h", tag="bank%d" % g)
+                    for s, t in enumerate(tiles):
+                        wc = slice(P * t, P * (t + 1))
+                        nc.tensor.matmul_mx(banks[g][:, s, :], lhsT=w_codes[:, wc].bitcast(FP8X4), lhsT_scale=w_plane[:, wc],
+                                            rhs=z_codes[:, gc].bitcast(FP8X4), rhs_scale=z_plane[:, gc], start=True, stop=True)
+                    for s, t in enumerate(tiles):
+                        nc.scalar.copy(hid[t][:, gc], banks[g][:, s, :])
+
+        y_codes = sb("y_codes", [P, S], U32)
+        y_plane = sb("y_plane", [P, S], U8)
+        out_rows = out_0.rearrange("(p t) j -> p t j", t=PACK)
+        out_words = out_1[0].rearrange("p n t -> p (n t)").bitcast(I32)
+        ys = {}
+        for g, (gc, tiles) in enumerate(groups):
+            n = gc.stop - gc.start
+            ts = slice(tiles[0], tiles[-1] + 1)
+            shape = [P, len(tiles), n]
+            h4 = sb("h4_%d" % g, shape, F32)
+            h5 = sb("h5_%d" % g, shape, F32)
+            pa = sb("pa%d" % g, shape, F32)
+            pb = sb("pb%d" % g, shape, F32)
+            mid = sb("mid%d" % g, shape, F32)
+            if gc.start not in ys:
+                ys[gc.start] = sb("y%d" % g, [P, PACK, n], F32)
+            y = ys[gc.start]
+            for s, t in enumerate(tiles):
+                fetch("s", h4[:, s, :], hid[t], n4_l, gc)
+            for s, t in enumerate(tiles):
+                fetch("v" if (g, t) == (0, 0) else "s", h5[:, s, :], hid[t], n5_l, gc)
+            nc.vector.tensor_tensor(pa[:], banks[g][:], h4[:], ALU.subtract)
+            nc.vector.tensor_tensor(pb[:], h5[:], banks[g][:], ALU.subtract)
+            nc.vector.scalar_tensor_tensor(mid[:], pb[:], 0.0, pa[:], ALU.min, ALU.max)
+            nc.vector.scalar_tensor_tensor(y[:, ts, :], pb[:], 0.0, mid[:], ALU.max, ALU.min)
+            nc.sync.dma_start(out_rows[:, ts, gc], y[:, ts, :])
+            if tiles[-1] == PACK - 1:
+                y_bf = sb("y_bf%d" % g, [P, n * PACK], BF16)
+                nc.vector.tensor_copy(y_bf[:].rearrange("p (c i t) -> p c t i", i=4, t=PACK),
+                                      y[:].rearrange("p t (c i) -> p c t i", i=4))
+                nc.vector.quantize_mx(y_codes[:, gc].bitcast(FP8X4), y_plane[:, gc], y_bf[:])
+                nc.sync.dma_start(out_words[:, gc], y_codes[:, gc].bitcast(I32))
+        for q in range(4):
+            engine = nc.sync if q % 2 == 0 else nc.scalar
+            engine.dma_start(out_2[0, 4 * q:4 * q + 4, :].bitcast(I32), y_plane[32 * q:32 * q + 4, :].bitcast(I32))

@@ -17,7 +17,6 @@ PACK = 4
 S = 512
 T = 1024
 G = 2048
-HALF = 256
 WIDE = 384
 PAD = 32
 FLOPS = 3 * 2 * 512 * 512 * 512
@@ -28,10 +27,14 @@ def tile_picked_twpqclampbminmod_none_po_kernel(tc, x_words, x_scales, d_words, 
     nc = tc.nc
     with ExitStack() as ctx:
         keep = ctx.enter_context(tc.tile_pool(name="keep", bufs=1))
+        turn = ctx.enter_context(tc.tile_pool(name="turn", bufs=1))
         psum = ctx.enter_context(tc.psum_pool(name="psum", bufs=1))
 
         def sb(name, shape, dtype, tag=None):
             return keep.tile(shape, dtype, name=name, tag=tag or name, align_bytes=64)
+
+        def at(name, shape, dtype, offset):
+            return turn.tile(shape, dtype, name=name, offset=offset, align_bytes=64)
 
         def load_list(name, src):
             tile = sb(name, [P, S // 16], U16)
@@ -50,33 +53,42 @@ def tile_picked_twpqclampbminmod_none_po_kernel(tc, x_words, x_scales, d_words, 
             return tile
 
         def deal_words(dst, src):
-            nc.vector.tensor_copy(dst.rearrange("p (t c i) -> p c t i", t=PACK, i=4),
-                                  src.rearrange("p (c i t) -> p c t i", t=PACK, i=4))
+            nc.vector.tensor_copy(dst[:].rearrange("p (t c i) -> p c t i", t=PACK, i=4),
+                                  src[:].rearrange("p (c i t) -> p c t i", t=PACK, i=4))
 
         def deal_bytes(dst, src):
             nc.vector.tensor_copy(dst.rearrange("p (t m) -> p t m", t=PACK),
                                   src.rearrange("p (m t) -> p t m", t=PACK))
 
+        def pick(dst, table, list_tile):
+            nc.vector.tensor_copy(dst[:], table[:].indirect(list_tile[:]))
+
+        def fetch(engine, dst, window, list_tile, cols):
+            picked = window[:].indirect(list_tile[:, cols.start // 16:cols.stop // 16])
+            if engine == "v":
+                nc.vector.tensor_copy(dst, picked)
+            else:
+                nc.scalar.activation(dst, picked, COPY)
+
         planes = [sb("plane%d" % e, [P, 2 * S], U8) for e in range(2)]
         w_rows = sb("w_rows", [P, S], U8)
         for tile in planes + [w_rows]:
             nc.gpsimd.memset(tile[:].bitcast(I32), 0)
-
         a = [sb("a%d" % t, [P, S + PAD], F32) for t in range(PACK)]
         b = [sb("b%d" % t, [P, S], F32) for t in range(PACK)]
         for t in range(PACK):
             nc.gpsimd.memset(a[t][:, S:], 0.0)
 
-        offs_l = load_list("offs_l", offs)
-        x_rows = load_scale_rows("x_rows", x_scales, T)
         k1_l = load_list("k1_l", k1)
         d_rows = load_scale_rows("d_rows", d_scales, G)
+        offs_l = load_list("offs_l", offs)
+        x_rows = load_scale_rows("x_rows", x_scales, T)
         x_tab = load_words("x_tab", x_words, T)
+        d_tab = load_words("d_tab", d_words, G)
         k2_l = load_list("k2_l", k2)
         two_l = load_list("two_l", two)
         n1_l = load_list("n1_l", n1)
         n2_l = load_list("n2_l", n2)
-        d_tab = load_words("d_tab", d_words, G)
         n3_l = load_list("n3_l", n3)
         n4_l = load_list("n4_l", n4)
         n5_l = load_list("n5_l", n5)
@@ -88,125 +100,183 @@ def tile_picked_twpqclampbminmod_none_po_kernel(tc, x_words, x_scales, d_words, 
         gain = sb("gain", [P, PACK], F32)
         nc.scalar.activation(gain[:], gain_raw[:], COPY, scale=0.0625)
 
-        def coded_product(e, k_l, x_l, rows, on_vector):
-            plane = planes[e]
-            g_b = sb("g_b%d" % e, [P, 2 * S], U8, "chain" if e else None)
+        def scale_plane(e, k_l, x_l, gd_b, gx_b, queue):
             side = sb("side%d" % e, [P, 2 * S], U8)
-            nc.vector.tensor_copy(g_b[:, S:], x_rows[:].indirect(x_l[:]))
-            nc.vector.tensor_copy(g_b[:, :S], d_rows[:].indirect(k_l[:]))
-            nc.vector.tensor_copy(side[:, S:].bitcast(I32), g_b[:, S:].bitcast(I32))
-            deal_bytes(side[:, :S], g_b[:, :S])
+            pick(gd_b, d_rows, k_l)
+            pick(gx_b, x_rows, x_l)
+            deal_bytes(side[:, :S], gd_b[:])
+            nc.vector.tensor_copy(side[:, S:].bitcast(I32), gx_b[:].bitcast(I32))
             for q in range(4):
-                nc.sync.dma_start(plane[32 * q:32 * q + 4, :].bitcast(I32),
-                                  side[32 * q:32 * q + 32:8, :].bitcast(I32))
-            if e == 0:
-                gx_w = sb("gx_w0", [P, S], U32)[:]
-                gd_w = sb("gd_w0", [P, S], U32, "chain")[:]
-            else:
-                g_w = sb("g_w1", [P, 2 * S], U32, "chain")
-                gx_w, gd_w = g_w[:, S:], g_w[:, :S]
+                queue.dma_start(planes[e][32 * q:32 * q + 4, :].bitcast(I32),
+                                side[32 * q:32 * q + 32:8, :].bitcast(I32))
+
+        def product(e, gd_w, gx_w, rows):
             dealt = sb("dealt%d" % e, [P, S], U32)
-            nc.vector.tensor_copy(gx_w, x_tab[:].indirect(x_l[:]))
-            nc.vector.tensor_copy(gd_w, d_tab[:].indirect(k_l[:]))
-            deal_words(dealt[:], gd_w)
+            deal_words(dealt, gd_w)
+            accs = []
             for t in range(PACK):
                 cols = slice(P * t, P * (t + 1))
                 acc = psum.tile([P, S], F32, name="acc", tag="bank%d" % (PACK * e + t))
-                nc.tensor.matmul_mx(acc[:], lhsT=dealt[:, cols].bitcast(FP8X4), lhsT_scale=plane[:, cols],
-                                    rhs=gx_w.bitcast(FP8X4), rhs_scale=plane[:, S:], start=True, stop=True)
-                if t in on_vector:
-                    nc.vector.tensor_copy(rows[t][:, :S], acc[:])
-                else:
-                    nc.scalar.copy(rows[t][:, :S], acc[:])
+                nc.tensor.matmul_mx(acc[:], lhsT=dealt[:, cols].bitcast(FP8X4), lhsT_scale=planes[e][:, cols],
+                                    rhs=gx_w[:].bitcast(FP8X4), rhs_scale=planes[e][:, S:], start=True, stop=True)
+                accs.append(acc)
+            return accs
 
-        def fetch(engine, dst, window, list_tile, cols):
-            picked = window[:].indirect(list_tile[:, cols.start // 16:cols.stop // 16])
-            if engine == "v":
-                nc.vector.tensor_copy(dst, picked)
-            else:
-                nc.scalar.activation(dst, picked, COPY)
-
-        coded_product(0, k1_l, offs_l, a, ())
-        a1 = sb("a_at_n1", [P, PACK, S], F32)
+        scale_plane(0, k1_l, offs_l, sb("gd_b0", [P, S], U8), sb("gx_b0", [P, S], U8), nc.scalar)
+        gx_w0 = sb("gx_w0", [P, S], U32, "gd_b0")
+        gd_w0 = at("gd_w0", [P, S], U32, 1024)
+        pick(gx_w0, x_tab, offs_l)
+        pick(gd_w0, d_tab, k1_l)
+        accs = product(0, gd_w0, gx_w0, a)
         for t in range(PACK):
-            fetch("s", a1[:, t, :], a[t], n1_l, slice(0, S))
-        coded_product(1, k2_l, two_l, b, (0, 1))
+            nc.scalar.copy(a[t][:, :S], accs[t][:])
+        a_n1 = sb("a_n1", [P, PACK, S], F32)
+        for t in range(PACK):
+            fetch("s", a_n1[:, t, :], a[t], n1_l, slice(0, S))
 
-        w_tab = load_words("w_tab", w1_words, S, "g_b0")
-        w_codes = sb("w_codes", [P, S], U32, "dealt0")
-        w_plane = sb("w_plane", [P, S], U8, "plane0")
-        deal_words(w_codes[:], w_tab[:])
+        scale_plane(1, k2_l, two_l, at("gd_b1", [P, S], U8, 1536), at("gx_b1", [P, S], U8, 2048), nc.sync)
+        gd_w1 = at("gd_w1", [P, S], U32, 0)
+        gx_w1 = at("gx_w1", [P, S], U32, 2048)
+        pick(gd_w1, d_tab, k2_l)
+        pick(gx_w1, x_tab, two_l)
+        accs = product(1, gd_w1, gx_w1, b)
+
+        w_tab = load_words("w_tab", w1_words, S, "side0")
+        w_codes = at("w_codes", [P, S], U32, 0)
+        w_plane = sb("w_plane", [P, S], U8, "side1")
+        deal_words(w_codes, w_tab)
         deal_bytes(w_plane[:], w_rows[:])
-
-        u = sb("u", [P, PACK, S], F32)
         for t in range(PACK):
-            nc.vector.scalar_tensor_tensor(u[:, t, :], a1[:, t, :], -0.5, a[t][:, :S], ALU.mult, ALU.add)
+            nc.vector.tensor_copy(b[t][:], accs[t][:])
 
-        hid = [sb("hid%d" % t, [P, S], F32) for t in range(PACK)]
+        u = at("u", [P, PACK, S], F32, 2048)
+        b2 = sb("b_n2", [P, PACK, S], F32)
+        b3 = sb("b_n3", [P, PACK, S], F32)
+        low = sb("low", [P, PACK, S], F32)
+        top = sb("top", [P, PACK, S], F32)
+        z = sb("z", [P, S * PACK], BF16)
         z_codes = sb("z_codes", [P, S], U32)
         z_plane = sb("z_plane", [P, S], U8)
-        groups = [(slice(0, 256), (0, 1)), (slice(0, 256), (2, 3)), (slice(256, 384), (0, 1, 2, 3)), (slice(384, 512), (0, 1, 2, 3))]
+        hid = [sb("hid%d" % t, [P, S], F32) for t in range(PACK)]
+        first, last = slice(0, WIDE), slice(WIDE, S)
+        front, back, every = slice(0, 2), slice(2, 4), slice(0, 4)
+        groups = [(slice(0, 256), front), (slice(0, 256), back), (slice(256, 384), every), (slice(384, 512), every)]
         banks = {}
-        for piece, cols in enumerate((slice(0, WIDE), slice(WIDE, S))):
+
+        def make_u(t):
+            nc.vector.scalar_tensor_tensor(u[:, t, :], a_n1[:, t, :], -0.5, a[t][:, :S], ALU.mult, ALU.add)
+
+        def make_low(ts, cols):
+            nc.vector.tensor_tensor(low[:, ts, cols], u[:, ts, cols], b2[:, ts, cols], ALU.min)
+
+        def make_top(ts, cols):
+            nc.vector.tensor_tensor(top[:, ts, cols], low[:, ts, cols], b3[:, ts, cols], ALU.max)
+
+        def make_z(cols):
             n = cols.stop - cols.start
-            b2 = sb("b2_%d" % piece, [P, PACK, n], F32)
-            b3 = sb("b3_%d" % piece, [P, PACK, n], F32)
-            low = sb("low%d" % piece, [P, PACK, n], F32)
-            top = sb("top%d" % piece, [P, PACK, n], F32)
-            for ts in ((slice(0, 2), slice(2, 4)) if piece == 0 else (slice(0, 4),)):
-                for t in range(ts.start, ts.stop):
-                    fetch("v" if (piece, t) == (0, 0) else "s", b2[:, t, :], b[t], n2_l, cols)
-                for t in range(ts.start, ts.stop):
-                    fetch("v" if (piece, t) == (0, 0) else "s", b3[:, t, :], b[t], n3_l, cols)
-                nc.vector.tensor_tensor(low[:, ts, :], u[:, ts, cols], b2[:, ts, :], ALU.min)
-                nc.vector.tensor_tensor(top[:, ts, :], low[:, ts, :], b3[:, ts, :], ALU.max)
-            z = sb("z%d" % piece, [P, n * PACK], BF16)
-            nc.vector.tensor_tensor(z[:].rearrange("p (c i t) -> p c t i", i=4, t=PACK),
-                                    top[:].rearrange("p t (c i) -> p c t i", i=4),
+            nc.vector.tensor_tensor(z[:, PACK * cols.start:PACK * cols.stop].rearrange("p (c i t) -> p c t i", i=4, t=PACK),
+                                    top[:, :, cols].rearrange("p t (c i) -> p c t i", i=4),
                                     gain[:].unsqueeze(1).unsqueeze(3).broadcast_to([P, n // 4, PACK, 4]), ALU.mult)
-            nc.vector.quantize_mx(z_codes[:, cols].bitcast(FP8X4), z_plane[:, cols], z[:])
-            for g, (gc, tiles) in enumerate(groups):
+
+        def dense(cols):
+            nc.vector.quantize_mx(z_codes[:, cols].bitcast(FP8X4), z_plane[:, cols], z[:, PACK * cols.start:PACK * cols.stop])
+            for g, (gc, ts) in enumerate(groups):
                 if cols.start <= gc.start and gc.stop <= cols.stop:
-                    banks[g] = psum.tile([P, len(tiles), gc.stop - gc.start], F32, name="acc_h", tag="bank%d" % g)
-                    for s, t in enumerate(tiles):
+                    banks[g] = psum.tile([P, ts.stop - ts.start, gc.stop - gc.start], F32, name="acc_h", tag="bank%d" % g)
+                    for t in range(ts.start, ts.stop):
                         wc = slice(P * t, P * (t + 1))
-                        nc.tensor.matmul_mx(banks[g][:, s, :], lhsT=w_codes[:, wc].bitcast(FP8X4), lhsT_scale=w_plane[:, wc],
-                                            rhs=z_codes[:, gc].bitcast(FP8X4), rhs_scale=z_plane[:, gc], start=True, stop=True)
-                    for s, t in enumerate(tiles):
-                        nc.scalar.copy(hid[t][:, gc], banks[g][:, s, :])
+                        nc.tensor.matmul_mx(banks[g][:, t - ts.start, :], lhsT=w_codes[:, wc].bitcast(FP8X4),
+                                            lhsT_scale=w_plane[:, wc], rhs=z_codes[:, gc].bitcast(FP8X4),
+                                            rhs_scale=z_plane[:, gc], start=True, stop=True)
+                    for t in range(ts.start, ts.stop):
+                        nc.scalar.copy(hid[t][:, gc], banks[g][:, t - ts.start, :])
+
+        for cols, pairs in ((first, (front, back)), (last, (every,))):
+            for ts in pairs:
+                for t in range(ts.start, ts.stop):
+                    fetch("s", b2[:, t, cols], b[t], n2_l, cols)
+                for t in range(ts.start, ts.stop):
+                    if (cols, t) != (first, 3):
+                        fetch("s", b3[:, t, cols], b[t], n3_l, cols)
+        left, right = slice(0, WIDE // 2), slice(WIDE // 2, WIDE)
+        make_u(0)
+        make_u(1)
+        make_u(2)
+        make_low(front, first)
+        make_u(3)
+        make_top(front, first)
+        fetch("v", b3[:, 3, first], b[3], n3_l, first)
+        make_low(back, left)
+        make_low(back, right)
+        make_top(back, left)
+        make_top(back, right)
+        make_z(left)
+        make_z(right)
+        make_low(every, last)
+        dense(first)
+        make_top(every, last)
+        make_z(last)
+        dense(last)
 
         y_codes = sb("y_codes", [P, S], U32)
         y_plane = sb("y_plane", [P, S], U8)
         out_rows = out_0.rearrange("(p t) j -> p t j", t=PACK)
         out_words = out_1[0].rearrange("p n t -> p (n t)").bitcast(I32)
-        ys = {}
-        for g, (gc, tiles) in enumerate(groups):
-            n = gc.stop - gc.start
-            ts = slice(tiles[0], tiles[-1] + 1)
-            shape = [P, len(tiles), n]
-            h4 = sb("h4_%d" % g, shape, F32)
-            h5 = sb("h5_%d" % g, shape, F32)
-            pa = sb("pa%d" % g, shape, F32)
-            pb = sb("pb%d" % g, shape, F32)
-            mid = sb("mid%d" % g, shape, F32)
-            if gc.start not in ys:
-                ys[gc.start] = sb("y%d" % g, [P, PACK, n], F32)
-            y = ys[gc.start]
-            for s, t in enumerate(tiles):
-                fetch("s", h4[:, s, :], hid[t], n4_l, gc)
-            for s, t in enumerate(tiles):
-                fetch("v" if (g, t) == (0, 0) else "s", h5[:, s, :], hid[t], n5_l, gc)
-            nc.vector.tensor_tensor(pa[:], banks[g][:], h4[:], ALU.subtract)
-            nc.vector.tensor_tensor(pb[:], h5[:], banks[g][:], ALU.subtract)
-            nc.vector.scalar_tensor_tensor(mid[:], pb[:], 0.0, pa[:], ALU.min, ALU.max)
-            nc.vector.scalar_tensor_tensor(y[:, ts, :], pb[:], 0.0, mid[:], ALU.max, ALU.min)
-            nc.sync.dma_start(out_rows[:, ts, gc], y[:, ts, :])
-            if tiles[-1] == PACK - 1:
-                y_bf = sb("y_bf%d" % g, [P, n * PACK], BF16)
-                nc.vector.tensor_copy(y_bf[:].rearrange("p (c i t) -> p c t i", i=4, t=PACK),
-                                      y[:].rearrange("p t (c i) -> p c t i", i=4))
-                nc.vector.quantize_mx(y_codes[:, gc].bitcast(FP8X4), y_plane[:, gc], y_bf[:])
-                nc.sync.dma_start(out_words[:, gc], y_codes[:, gc].bitcast(I32))
+        h4 = sb("h4", [P, PACK, S], F32)
+        h5 = sb("h5", [P, PACK, S], F32)
+        pa = sb("pa", [P, PACK, S], F32)
+        pb = sb("pb", [P, PACK, S], F32)
+        mid = sb("mid", [P, PACK, S], F32)
+        y = sb("y", [P, PACK, S], F32)
+        y_bf = sb("y_bf", [P, S * PACK], BF16)
+        for g, (gc, ts) in enumerate(groups):
+            for t in range(ts.start, ts.stop):
+                fetch("s", h4[:, t, gc], hid[t], n4_l, gc)
+            for t in range(ts.start, ts.stop):
+                fetch("v" if g == 0 else "s", h5[:, t, gc], hid[t], n5_l, gc)
+
+        def make_pa(g):
+            gc, ts = groups[g]
+            nc.vector.tensor_tensor(pa[:, ts, gc], banks[g][:], h4[:, ts, gc], ALU.subtract)
+
+        def make_pb(g):
+            gc, ts = groups[g]
+            nc.vector.tensor_tensor(pb[:, ts, gc], h5[:, ts, gc], banks[g][:], ALU.subtract)
+
+        def make_mid(g):
+            gc, ts = groups[g]
+            nc.vector.scalar_tensor_tensor(mid[:, ts, gc], pb[:, ts, gc], 0.0, pa[:, ts, gc], ALU.min, ALU.max)
+
+        def make_y(g):
+            gc, ts = groups[g]
+            nc.vector.scalar_tensor_tensor(y[:, ts, gc], pb[:, ts, gc], 0.0, mid[:, ts, gc], ALU.max, ALU.min)
+            nc.sync.dma_start(out_rows[:, ts, gc], y[:, ts, gc])
+
+        def round_y(copy, g):
+            gc = groups[g][0]
+            copy(y_bf[:, PACK * gc.start:PACK * gc.stop].rearrange("p (c i t) -> p c t i", i=4, t=PACK),
+                 y[:, :, gc].rearrange("p t (c i) -> p c t i", i=4))
+
+        def pack_y(g):
+            gc = groups[g][0]
+            nc.vector.quantize_mx(y_codes[:, gc].bitcast(FP8X4), y_plane[:, gc], y_bf[:, PACK * gc.start:PACK * gc.stop])
+            nc.sync.dma_start(out_words[:, gc], y_codes[:, gc].bitcast(I32))
+
+        make_pb(0)
+        make_pa(0)
+        for g in range(1, 4):
+            make_pa(g)
+            make_mid(g - 1)
+            make_pb(g)
+            make_y(g - 1)
+        round_y(nc.scalar.copy, 1)
+        make_mid(3)
+        round_y(nc.vector.tensor_copy, 2)
+        make_y(3)
+        pack_y(2)
+        pack_y(1)
+        round_y(nc.vector.tensor_copy, 3)
+        pack_y(3)
         for q in range(4):
             engine = nc.sync if q % 2 == 0 else nc.scalar
             engine.dma_start(out_2[0, 4 * q:4 * q + 4, :].bitcast(I32), y_plane[32 * q:32 * q + 4, :].bitcast(I32))

@@ -14,15 +14,18 @@ COPY = mybir.ActivationFunctionType.Copy
 
 P = 128
 PACK = 4
+QUADRANTS = 4
 S = 512
 T = 1024
 G = 2048
+LINE = 4
 WIDE = 384
 PAD = 32
 FLOPS = 3 * 2 * 512 * 512 * 512
 
 
-def tile_picked_twpqclampbminmod_none_po_kernel(tc, x_words, x_scales, d_words, d_scales, gn, w1_words, w1_scales,
+def tile_picked_twpqclampbminmod_none_po_kernel(
+        tc, x_words, x_scales, d_words, d_scales, gn, w1_words, w1_scales,
         offs, k1, two, k2, n1, n2, n3, n4, n5, out_0, out_1, out_2):
     nc = tc.nc
     with ExitStack() as ctx:
@@ -53,8 +56,8 @@ def tile_picked_twpqclampbminmod_none_po_kernel(tc, x_words, x_scales, d_words, 
             return tile
 
         def deal_words(dst, src):
-            nc.vector.tensor_copy(dst[:].rearrange("p (t c i) -> p c t i", t=PACK, i=4),
-                                  src[:].rearrange("p (c i t) -> p c t i", t=PACK, i=4))
+            nc.vector.tensor_copy(dst[:].rearrange("p (t c i) -> p c t i", t=PACK, i=LINE),
+                                  src[:].rearrange("p (c i t) -> p c t i", t=PACK, i=LINE))
 
         def deal_bytes(dst, src):
             nc.vector.tensor_copy(dst.rearrange("p (t m) -> p t m", t=PACK),
@@ -63,12 +66,18 @@ def tile_picked_twpqclampbminmod_none_po_kernel(tc, x_words, x_scales, d_words, 
         def pick(dst, table, list_tile):
             nc.vector.tensor_copy(dst[:], table[:].indirect(list_tile[:]))
 
-        def fetch(engine, dst, window, list_tile, cols):
+        def fetch(on_vector, dst, window, list_tile, cols):
             picked = window[:].indirect(list_tile[:, cols.start // 16:cols.stop // 16])
-            if engine == "v":
+            if on_vector:
                 nc.vector.tensor_copy(dst, picked)
             else:
                 nc.scalar.activation(dst, picked, COPY)
+
+        def woven(tile, cols):
+            return tile[:, PACK * cols.start:PACK * cols.stop].rearrange("p (c i t) -> p c t i", i=LINE, t=PACK)
+
+        def by_lines(tile, cols):
+            return tile[:, :, cols].rearrange("p t (c i) -> p c t i", i=LINE)
 
         planes = [sb("plane%d" % e, [P, 2 * S], U8) for e in range(2)]
         w_rows = sb("w_rows", [P, S], U8)
@@ -84,18 +93,18 @@ def tile_picked_twpqclampbminmod_none_po_kernel(tc, x_words, x_scales, d_words, 
         offs_l = load_list("offs_l", offs)
         x_rows = load_scale_rows("x_rows", x_scales, T)
         x_tab = load_words("x_tab", x_words, T)
-        d_tab = load_words("d_tab", d_words, G)
         k2_l = load_list("k2_l", k2)
         two_l = load_list("two_l", two)
         n1_l = load_list("n1_l", n1)
         n2_l = load_list("n2_l", n2)
+        d_tab = load_words("d_tab", d_words, G)
         n3_l = load_list("n3_l", n3)
         n4_l = load_list("n4_l", n4)
         n5_l = load_list("n5_l", n5)
 
         gain_raw = sb("gain_raw", [P, PACK], F32)
         nc.gpsimd.dma_start(gain_raw[:], gn.rearrange("(p t) o -> p (t o)", t=PACK))
-        for q in range(4):
+        for q in range(QUADRANTS):
             nc.gpsimd.dma_start(w_rows[32 * q:32 * q + 4, :].bitcast(I32), w1_scales[0, 4 * q:4 * q + 4, :].bitcast(I32))
         gain = sb("gain", [P, PACK], F32)
         nc.scalar.activation(gain[:], gain_raw[:], COPY, scale=0.0625)
@@ -106,11 +115,11 @@ def tile_picked_twpqclampbminmod_none_po_kernel(tc, x_words, x_scales, d_words, 
             pick(gx_b, x_rows, x_l)
             deal_bytes(side[:, :S], gd_b[:])
             nc.vector.tensor_copy(side[:, S:].bitcast(I32), gx_b[:].bitcast(I32))
-            for q in range(4):
+            for q in range(QUADRANTS):
                 queue.dma_start(planes[e][32 * q:32 * q + 4, :].bitcast(I32),
                                 side[32 * q:32 * q + 32:8, :].bitcast(I32))
 
-        def product(e, gd_w, gx_w, rows):
+        def product(e, gd_w, gx_w):
             dealt = sb("dealt%d" % e, [P, S], U32)
             deal_words(dealt, gd_w)
             accs = []
@@ -122,24 +131,25 @@ def tile_picked_twpqclampbminmod_none_po_kernel(tc, x_words, x_scales, d_words, 
                 accs.append(acc)
             return accs
 
+        W = 4 * S
         scale_plane(0, k1_l, offs_l, sb("gd_b0", [P, S], U8), sb("gx_b0", [P, S], U8), nc.scalar)
         gx_w0 = sb("gx_w0", [P, S], U32, "gd_b0")
-        gd_w0 = at("gd_w0", [P, S], U32, 1024)
+        gd_w0 = at("gd_w0", [P, S], U32, W // 2)
         pick(gx_w0, x_tab, offs_l)
         pick(gd_w0, d_tab, k1_l)
-        accs = product(0, gd_w0, gx_w0, a)
+        accs = product(0, gd_w0, gx_w0)
         for t in range(PACK):
             nc.scalar.copy(a[t][:, :S], accs[t][:])
         a_n1 = sb("a_n1", [P, PACK, S], F32)
         for t in range(PACK):
-            fetch("s", a_n1[:, t, :], a[t], n1_l, slice(0, S))
+            fetch(False, a_n1[:, t, :], a[t], n1_l, slice(0, S))
 
-        scale_plane(1, k2_l, two_l, at("gd_b1", [P, S], U8, 1536), at("gx_b1", [P, S], U8, 2048), nc.sync)
+        scale_plane(1, k2_l, two_l, at("gd_b1", [P, S], U8, W - S), at("gx_b1", [P, S], U8, W), nc.sync)
         gd_w1 = at("gd_w1", [P, S], U32, 0)
-        gx_w1 = at("gx_w1", [P, S], U32, 2048)
+        gx_w1 = at("gx_w1", [P, S], U32, W)
         pick(gd_w1, d_tab, k2_l)
         pick(gx_w1, x_tab, two_l)
-        accs = product(1, gd_w1, gx_w1, b)
+        accs = product(1, gd_w1, gx_w1)
 
         w_tab = load_words("w_tab", w1_words, S, "side0")
         w_codes = at("w_codes", [P, S], U32, 0)
@@ -149,34 +159,33 @@ def tile_picked_twpqclampbminmod_none_po_kernel(tc, x_words, x_scales, d_words, 
         for t in range(PACK):
             nc.vector.tensor_copy(b[t][:], accs[t][:])
 
-        u = at("u", [P, PACK, S], F32, 2048)
-        b2 = sb("b_n2", [P, PACK, S], F32)
-        b3 = sb("b_n3", [P, PACK, S], F32)
+        u = at("u", [P, PACK, S], F32, W)
+        b_n2 = sb("b_n2", [P, PACK, S], F32)
+        b_n3 = sb("b_n3", [P, PACK, S], F32)
         low = sb("low", [P, PACK, S], F32)
         top = sb("top", [P, PACK, S], F32)
         z = sb("z", [P, S * PACK], BF16)
         z_codes = sb("z_codes", [P, S], U32)
         z_plane = sb("z_plane", [P, S], U8)
-        hid = [sb("hid%d" % t, [P, S], F32) for t in range(PACK)]
+        h = [sb("h_row%d" % t, [P, S], F32) for t in range(PACK)]
         first, last = slice(0, WIDE), slice(WIDE, S)
         front, back, every = slice(0, 2), slice(2, 4), slice(0, 4)
-        groups = [(slice(0, 256), front), (slice(0, 256), back), (slice(256, 384), every), (slice(384, 512), every)]
+        groups = [(slice(0, S // 2), front), (slice(0, S // 2), back), (slice(S // 2, WIDE), every), (last, every)]
         banks = {}
 
         def make_u(t):
             nc.vector.scalar_tensor_tensor(u[:, t, :], a_n1[:, t, :], -0.5, a[t][:, :S], ALU.mult, ALU.add)
 
         def make_low(ts, cols):
-            nc.vector.tensor_tensor(low[:, ts, cols], u[:, ts, cols], b2[:, ts, cols], ALU.min)
+            nc.vector.tensor_tensor(low[:, ts, cols], u[:, ts, cols], b_n2[:, ts, cols], ALU.min)
 
         def make_top(ts, cols):
-            nc.vector.tensor_tensor(top[:, ts, cols], low[:, ts, cols], b3[:, ts, cols], ALU.max)
+            nc.vector.tensor_tensor(top[:, ts, cols], low[:, ts, cols], b_n3[:, ts, cols], ALU.max)
 
         def make_z(cols):
-            n = cols.stop - cols.start
-            nc.vector.tensor_tensor(z[:, PACK * cols.start:PACK * cols.stop].rearrange("p (c i t) -> p c t i", i=4, t=PACK),
-                                    top[:, :, cols].rearrange("p t (c i) -> p c t i", i=4),
-                                    gain[:].unsqueeze(1).unsqueeze(3).broadcast_to([P, n // 4, PACK, 4]), ALU.mult)
+            runs = (cols.stop - cols.start) // LINE
+            nc.vector.tensor_tensor(woven(z, cols), by_lines(top, cols),
+                                    gain[:].unsqueeze(1).unsqueeze(3).broadcast_to([P, runs, PACK, LINE]), ALU.mult)
 
         def dense(cols):
             nc.vector.quantize_mx(z_codes[:, cols].bitcast(FP8X4), z_plane[:, cols], z[:, PACK * cols.start:PACK * cols.stop])
@@ -189,15 +198,15 @@ def tile_picked_twpqclampbminmod_none_po_kernel(tc, x_words, x_scales, d_words, 
                                             lhsT_scale=w_plane[:, wc], rhs=z_codes[:, gc].bitcast(FP8X4),
                                             rhs_scale=z_plane[:, gc], start=True, stop=True)
                     for t in range(ts.start, ts.stop):
-                        nc.scalar.copy(hid[t][:, gc], banks[g][:, t - ts.start, :])
+                        nc.scalar.copy(h[t][:, gc], banks[g][:, t - ts.start, :])
 
         for cols, pairs in ((first, (front, back)), (last, (every,))):
             for ts in pairs:
                 for t in range(ts.start, ts.stop):
-                    fetch("s", b2[:, t, cols], b[t], n2_l, cols)
+                    fetch(False, b_n2[:, t, cols], b[t], n2_l, cols)
                 for t in range(ts.start, ts.stop):
-                    if (cols, t) != (first, 3):
-                        fetch("s", b3[:, t, cols], b[t], n3_l, cols)
+                    if (cols, t) != (first, PACK - 1):
+                        fetch(False, b_n3[:, t, cols], b[t], n3_l, cols)
         left, right = slice(0, WIDE // 2), slice(WIDE // 2, WIDE)
         make_u(0)
         make_u(1)
@@ -205,7 +214,7 @@ def tile_picked_twpqclampbminmod_none_po_kernel(tc, x_words, x_scales, d_words, 
         make_low(front, first)
         make_u(3)
         make_top(front, first)
-        fetch("v", b3[:, 3, first], b[3], n3_l, first)
+        fetch(True, b_n3[:, PACK - 1, first], b[PACK - 1], n3_l, first)
         make_low(back, left)
         make_low(back, right)
         make_top(back, left)
@@ -214,7 +223,8 @@ def tile_picked_twpqclampbminmod_none_po_kernel(tc, x_words, x_scales, d_words, 
         make_z(right)
         make_low(every, last)
         dense(first)
-        make_top(every, last)
+        make_top(front, last)
+        make_top(back, last)
         make_z(last)
         dense(last)
 
@@ -222,8 +232,8 @@ def tile_picked_twpqclampbminmod_none_po_kernel(tc, x_words, x_scales, d_words, 
         y_plane = sb("y_plane", [P, S], U8)
         out_rows = out_0.rearrange("(p t) j -> p t j", t=PACK)
         out_words = out_1[0].rearrange("p n t -> p (n t)").bitcast(I32)
-        h4 = sb("h4", [P, PACK, S], F32)
-        h5 = sb("h5", [P, PACK, S], F32)
+        h_n4 = sb("h_n4", [P, PACK, S], F32)
+        h_n5 = sb("h_n5", [P, PACK, S], F32)
         pa = sb("pa", [P, PACK, S], F32)
         pb = sb("pb", [P, PACK, S], F32)
         mid = sb("mid", [P, PACK, S], F32)
@@ -231,17 +241,17 @@ def tile_picked_twpqclampbminmod_none_po_kernel(tc, x_words, x_scales, d_words, 
         y_bf = sb("y_bf", [P, S * PACK], BF16)
         for g, (gc, ts) in enumerate(groups):
             for t in range(ts.start, ts.stop):
-                fetch("s", h4[:, t, gc], hid[t], n4_l, gc)
+                fetch(False, h_n4[:, t, gc], h[t], n4_l, gc)
             for t in range(ts.start, ts.stop):
-                fetch("v" if g == 0 else "s", h5[:, t, gc], hid[t], n5_l, gc)
+                fetch(g == 0, h_n5[:, t, gc], h[t], n5_l, gc)
 
         def make_pa(g):
             gc, ts = groups[g]
-            nc.vector.tensor_tensor(pa[:, ts, gc], banks[g][:], h4[:, ts, gc], ALU.subtract)
+            nc.vector.tensor_tensor(pa[:, ts, gc], banks[g][:], h_n4[:, ts, gc], ALU.subtract)
 
         def make_pb(g):
             gc, ts = groups[g]
-            nc.vector.tensor_tensor(pb[:, ts, gc], h5[:, ts, gc], banks[g][:], ALU.subtract)
+            nc.vector.tensor_tensor(pb[:, ts, gc], h_n5[:, ts, gc], banks[g][:], ALU.subtract)
 
         def make_mid(g):
             gc, ts = groups[g]
@@ -254,29 +264,29 @@ def tile_picked_twpqclampbminmod_none_po_kernel(tc, x_words, x_scales, d_words, 
 
         def round_y(copy, g):
             gc = groups[g][0]
-            copy(y_bf[:, PACK * gc.start:PACK * gc.stop].rearrange("p (c i t) -> p c t i", i=4, t=PACK),
-                 y[:, :, gc].rearrange("p t (c i) -> p c t i", i=4))
+            copy(woven(y_bf, gc), by_lines(y, gc))
 
         def pack_y(g):
             gc = groups[g][0]
             nc.vector.quantize_mx(y_codes[:, gc].bitcast(FP8X4), y_plane[:, gc], y_bf[:, PACK * gc.start:PACK * gc.stop])
             nc.sync.dma_start(out_words[:, gc], y_codes[:, gc].bitcast(I32))
 
+        end = len(groups) - 1
         make_pb(0)
         make_pa(0)
-        for g in range(1, 4):
+        for g in range(1, end + 1):
             make_pa(g)
             make_mid(g - 1)
             make_pb(g)
             make_y(g - 1)
-        round_y(nc.scalar.copy, 1)
-        make_mid(3)
-        round_y(nc.vector.tensor_copy, 2)
-        make_y(3)
-        pack_y(2)
-        pack_y(1)
-        round_y(nc.vector.tensor_copy, 3)
-        pack_y(3)
-        for q in range(4):
-            engine = nc.sync if q % 2 == 0 else nc.scalar
-            engine.dma_start(out_2[0, 4 * q:4 * q + 4, :].bitcast(I32), y_plane[32 * q:32 * q + 4, :].bitcast(I32))
+        round_y(nc.scalar.copy, end - 2)
+        round_y(nc.scalar.copy, end - 1)
+        make_mid(end)
+        pack_y(end - 2)
+        make_y(end)
+        pack_y(end - 1)
+        round_y(nc.vector.tensor_copy, end)
+        pack_y(end)
+        for q in range(QUADRANTS):
+            queue = nc.sync if q % 2 == 0 else nc.scalar
+            queue.dma_start(out_2[0, 4 * q:4 * q + 4, :].bitcast(I32), y_plane[32 * q:32 * q + 4, :].bitcast(I32))

from contextlib import ExitStack

import concourse.mybir as mybir

F32 = mybir.dt.float32
BF16 = mybir.dt.bfloat16
U32 = mybir.dt.uint32
I32 = mybir.dt.int32
U16 = mybir.dt.uint16
U8 = mybir.dt.uint8
FP8X4 = mybir.dt.float8_e4m3fn_x4
ALU = mybir.AluOpType
COPY = mybir.ActivationFunctionType.Copy

P = 128
PACK = 4
QUADRANTS = 4
S = 512
T = 1024
G = 2048
LINE = 4
WIDE = 384
PAD = 32
FLOPS = 3 * 2 * 512 * 512 * 512


def tile_picked_twpqclampbminmod_none_po_kernel(
        tc, x_words, x_scales, d_words, d_scales, gn, w1_words, w1_scales,
        offs, k1, two, k2, n1, n2, n3, n4, n5, out_0, out_1, out_2):
    nc = tc.nc
    with ExitStack() as ctx:
        keep = ctx.enter_context(tc.tile_pool(name="keep", bufs=1))
        turn = ctx.enter_context(tc.tile_pool(name="turn", bufs=1))
        psum = ctx.enter_context(tc.psum_pool(name="psum", bufs=1))

        def sb(name, shape, dtype, tag=None):
            return keep.tile(shape, dtype, name=name, tag=tag or name, align_bytes=64)

        def at(name, shape, dtype, offset):
            return turn.tile(shape, dtype, name=name, offset=offset, align_bytes=64)

        def load_list(name, src):
            tile = sb(name, [P, S // 16], U16)
            nc.sync.dma_start(tile[:], src)
            return tile

        def load_words(name, src, cols, tag=None):
            tile = sb(name, [P, cols], U32, tag)
            nc.sync.dma_start(tile[:].bitcast(I32), src[0].rearrange("p n t -> p (n t)").bitcast(I32))
            return tile

        def load_scale_rows(name, src, cols):
            tile = sb(name, [P, cols], U8)
            rows = src[0].bitcast(I32).unsqueeze(1).broadcast_to([16, 8, cols // 4])
            nc.sync.dma_start(tile[:].bitcast(I32), rows)
            return tile

        def deal_words(dst, src):
            nc.vector.tensor_copy(dst[:].rearrange("p (t c i) -> p c t i", t=PACK, i=LINE),
                                  src[:].rearrange("p (c i t) -> p c t i", t=PACK, i=LINE))

        def deal_bytes(dst, src):
            nc.vector.tensor_copy(dst.rearrange("p (t m) -> p t m", t=PACK),
                                  src.rearrange("p (m t) -> p t m", t=PACK))

        def pick(dst, table, list_tile):
            nc.vector.tensor_copy(dst[:], table[:].indirect(list_tile[:]))

        def fetch(on_vector, dst, window, list_tile, cols):
            picked = window[:].indirect(list_tile[:, cols.start // 16:cols.stop // 16])
            if on_vector:
                nc.vector.tensor_copy(dst, picked)
            else:
                nc.scalar.activation(dst, picked, COPY)

        def woven(tile, cols):
            return tile[:, PACK * cols.start:PACK * cols.stop].rearrange("p (c i t) -> p c t i", i=LINE, t=PACK)

        def by_lines(tile, cols):
            return tile[:, :, cols].rearrange("p t (c i) -> p c t i", i=LINE)

        planes = [sb("plane%d" % e, [P, 2 * S], U8) for e in range(2)]
        w_rows = sb("w_rows", [P, S], U8)
        for tile in planes + [w_rows]:
            nc.gpsimd.memset(tile[:].bitcast(I32), 0)
        a = [sb("a%d" % t, [P, S + PAD], F32) for t in range(PACK)]
        b = [sb("b%d" % t, [P, S], F32) for t in range(PACK)]
        for t in range(PACK):
            nc.gpsimd.memset(a[t][:, S:], 0.0)

        k1_l = load_list("k1_l", k1)
        d_rows = load_scale_rows("d_rows", d_scales, G)
        offs_l = load_list("offs_l", offs)
        x_rows = load_scale_rows("x_rows", x_scales, T)
        x_tab = load_words("x_tab", x_words, T)
        k2_l = load_list("k2_l", k2)
        two_l = load_list("two_l", two)
        n1_l = load_list("n1_l", n1)
        n2_l = load_list("n2_l", n2)
        d_tab = load_words("d_tab", d_words, G)
        n3_l = load_list("n3_l", n3)
        n4_l = load_list("n4_l", n4)
        n5_l = load_list("n5_l", n5)

        gain_raw = sb("gain_raw", [P, PACK], F32)
        nc.gpsimd.dma_start(gain_raw[:], gn.rearrange("(p t) o -> p (t o)", t=PACK))
        for q in range(QUADRANTS):
            nc.gpsimd.dma_start(w_rows[32 * q:32 * q + 4, :].bitcast(I32), w1_scales[0, 4 * q:4 * q + 4, :].bitcast(I32))
        gain = sb("gain", [P, PACK], F32)
        nc.scalar.activation(gain[:], gain_raw[:], COPY, scale=0.0625)

        def scale_plane(e, k_l, x_l, gd_b, gx_b, queue):
            side = sb("side%d" % e, [P, 2 * S], U8)
            pick(gd_b, d_rows, k_l)
            pick(gx_b, x_rows, x_l)
            deal_bytes(side[:, :S], gd_b[:])
            nc.vector.tensor_copy(side[:, S:].bitcast(I32), gx_b[:].bitcast(I32))
            for q in range(QUADRANTS):
                queue.dma_start(planes[e][32 * q:32 * q + 4, :].bitcast(I32),
                                side[32 * q:32 * q + 32:8, :].bitcast(I32))

        def product(e, gd_w, gx_w):
            dealt = sb("dealt%d" % e, [P, S], U32)
            deal_words(dealt, gd_w)
            accs = []
            for t in range(PACK):
                cols = slice(P * t, P * (t + 1))
                acc = psum.tile([P, S], F32, name="acc", tag="bank%d" % (PACK * e + t))
                nc.tensor.matmul_mx(acc[:], lhsT=dealt[:, cols].bitcast(FP8X4), lhsT_scale=planes[e][:, cols],
                                    rhs=gx_w[:].bitcast(FP8X4), rhs_scale=planes[e][:, S:], start=True, stop=True)
                accs.append(acc)
            return accs

        W = 4 * S
        scale_plane(0, k1_l, offs_l, sb("gd_b0", [P, S], U8), sb("gx_b0", [P, S], U8), nc.scalar)
        gx_w0 = sb("gx_w0", [P, S], U32, "gd_b0")
        gd_w0 = at("gd_w0", [P, S], U32, W // 2)
        pick(gx_w0, x_tab, offs_l)
        pick(gd_w0, d_tab, k1_l)
        accs = product(0, gd_w0, gx_w0)
        for t in range(PACK):
            nc.scalar.copy(a[t][:, :S], accs[t][:])
        a_n1 = sb("a_n1", [P, PACK, S], F32)
        for t in range(PACK):
            fetch(False, a_n1[:, t, :], a[t], n1_l, slice(0, S))

        scale_plane(1, k2_l, two_l, at("gd_b1", [P, S], U8, W - S), at("gx_b1", [P, S], U8, W), nc.sync)
        gd_w1 = at("gd_w1", [P, S], U32, 0)
        gx_w1 = at("gx_w1", [P, S], U32, W)
        pick(gd_w1, d_tab, k2_l)
        pick(gx_w1, x_tab, two_l)
        accs = product(1, gd_w1, gx_w1)

        w_tab = load_words("w_tab", w1_words, S, "side0")
        w_codes = at("w_codes", [P, S], U32, 0)
        w_plane = sb("w_plane", [P, S], U8, "side1")
        deal_words(w_codes, w_tab)
        deal_bytes(w_plane[:], w_rows[:])
        for t in range(PACK):
            nc.vector.tensor_copy(b[t][:], accs[t][:])

        u = at("u", [P, PACK, S], F32, W)
        b_n2 = sb("b_n2", [P, PACK, S], F32)
        b_n3 = sb("b_n3", [P, PACK, S], F32)
        low = sb("low", [P, PACK, S], F32)
        top = sb("top", [P, PACK, S], F32)
        z = sb("z", [P, S * PACK], BF16)
        z_codes = sb("z_codes", [P, S], U32)
        z_plane = sb("z_plane", [P, S], U8)
        h = [sb("h_row%d" % t, [P, S], F32) for t in range(PACK)]
        first, last = slice(0, WIDE), slice(WIDE, S)
        front, back, every = slice(0, 2), slice(2, 4), slice(0, 4)
        groups = [(slice(0, S // 2), front), (slice(0, S // 2), back), (slice(S // 2, WIDE), every), (last, every)]
        banks = {}

        def make_u(t):
            nc.vector.scalar_tensor_tensor(u[:, t, :], a_n1[:, t, :], -0.5, a[t][:, :S], ALU.mult, ALU.add)

        def make_low(ts, cols):
            nc.vector.tensor_tensor(low[:, ts, cols], u[:, ts, cols], b_n2[:, ts, cols], ALU.min)

        def make_top(ts, cols):
            nc.vector.tensor_tensor(top[:, ts, cols], low[:, ts, cols], b_n3[:, ts, cols], ALU.max)

        def make_z(cols):
            runs = (cols.stop - cols.start) // LINE
            nc.vector.tensor_tensor(woven(z, cols), by_lines(top, cols),
                                    gain[:].unsqueeze(1).unsqueeze(3).broadcast_to([P, runs, PACK, LINE]), ALU.mult)

        def dense(cols):
            nc.vector.quantize_mx(z_codes[:, cols].bitcast(FP8X4), z_plane[:, cols], z[:, PACK * cols.start:PACK * cols.stop])
            for g, (gc, ts) in enumerate(groups):
                if cols.start <= gc.start and gc.stop <= cols.stop:
                    banks[g] = psum.tile([P, ts.stop - ts.start, gc.stop - gc.start], F32, name="acc_h", tag="bank%d" % g)
                    for t in range(ts.start, ts.stop):
                        wc = slice(P * t, P * (t + 1))
                        nc.tensor.matmul_mx(banks[g][:, t - ts.start, :], lhsT=w_codes[:, wc].bitcast(FP8X4),
                                            lhsT_scale=w_plane[:, wc], rhs=z_codes[:, gc].bitcast(FP8X4),
                                            rhs_scale=z_plane[:, gc], start=True, stop=True)
                    for t in range(ts.start, ts.stop):
                        nc.scalar.copy(h[t][:, gc], banks[g][:, t - ts.start, :])

        for cols, pairs in ((first, (front, back)), (last, (every,))):
            for ts in pairs:
                for t in range(ts.start, ts.stop):
                    fetch(False, b_n2[:, t, cols], b[t], n2_l, cols)
                for t in range(ts.start, ts.stop):
                    if (cols, t) != (first, PACK - 1):
                        fetch(False, b_n3[:, t, cols], b[t], n3_l, cols)
        left, right = slice(0, WIDE // 2), slice(WIDE // 2, WIDE)
        make_u(0)
        make_u(1)
        make_u(2)
        make_low(front, first)
        make_u(3)
        make_top(front, first)
        fetch(True, b_n3[:, PACK - 1, first], b[PACK - 1], n3_l, first)
        make_low(back, left)
        make_low(back, right)
        make_top(back, left)
        make_top(back, right)
        make_z(left)
        make_z(right)
        make_low(every, last)
        dense(first)
        make_top(front, last)
        make_top(back, last)
        make_z(last)
        dense(last)

        y_codes = sb("y_codes", [P, S], U32)
        y_plane = sb("y_plane", [P, S], U8)
        out_rows = out_0.rearrange("(p t) j -> p t j", t=PACK)
        out_words = out_1[0].rearrange("p n t -> p (n t)").bitcast(I32)
        h_n4 = sb("h_n4", [P, PACK, S], F32)
        h_n5 = sb("h_n5", [P, PACK, S], F32)
        pa = sb("pa", [P, PACK, S], F32)
        pb = sb("pb", [P, PACK, S], F32)
        mid = sb("mid", [P, PACK, S], F32)
        y = sb("y", [P, PACK, S], F32)
        y_bf = sb("y_bf", [P, S * PACK], BF16)
        for g, (gc, ts) in enumerate(groups):
            for t in range(ts.start, ts.stop):
                fetch(False, h_n4[:, t, gc], h[t], n4_l, gc)
            for t in range(ts.start, ts.stop):
                fetch(g == 0, h_n5[:, t, gc], h[t], n5_l, gc)

        def make_pa(g):
            gc, ts = groups[g]
            nc.vector.tensor_tensor(pa[:, ts, gc], banks[g][:], h_n4[:, ts, gc], ALU.subtract)

        def make_pb(g):
            gc, ts = groups[g]
            nc.vector.tensor_tensor(pb[:, ts, gc], h_n5[:, ts, gc], banks[g][:], ALU.subtract)

        def make_mid(g):
            gc, ts = groups[g]
            nc.vector.scalar_tensor_tensor(mid[:, ts, gc], pb[:, ts, gc], 0.0, pa[:, ts, gc], ALU.min, ALU.max)

        def make_y(g):
            gc, ts = groups[g]
            nc.vector.scalar_tensor_tensor(y[:, ts, gc], pb[:, ts, gc], 0.0, mid[:, ts, gc], ALU.max, ALU.min)
            nc.sync.dma_start(out_rows[:, ts, gc], y[:, ts, gc])

        def round_y(copy, g):
            gc = groups[g][0]
            copy(woven(y_bf, gc), by_lines(y, gc))

        def pack_y(g):
            gc = groups[g][0]
            nc.vector.quantize_mx(y_codes[:, gc].bitcast(FP8X4), y_plane[:, gc], y_bf[:, PACK * gc.start:PACK * gc.stop])
            nc.sync.dma_start(out_words[:, gc], y_codes[:, gc].bitcast(I32))

        end = len(groups) - 1
        make_pb(0)
        make_pa(0)
        for g in range(1, end + 1):
            make_pa(g)
            make_mid(g - 1)
            make_pb(g)
            make_y(g - 1)
        round_y(nc.scalar.copy, end - 2)
        round_y(nc.scalar.copy, end - 1)
        make_mid(end)
        pack_y(end - 2)
        make_y(end)
        pack_y(end - 1)
        round_y(nc.vector.tensor_copy, end)
        pack_y(end)
        for q in range(QUADRANTS):
            queue = nc.sync if q % 2 == 0 else nc.scalar
            queue.dma_start(out_2[0, 4 * q:4 * q + 4, :].bitcast(I32), y_plane[32 * q:32 * q + 4, :].bitcast(I32))
